import numpy as np, ml_dtypes
CORES = [52,68,84,180,196,212,308,324,340]
N = 9
import mx_ref
NC, G = 128, 4
C = np.float32(0.041)
BF = ml_dtypes.bfloat16
def tile(rs):
    return np.stack(rs, axis=2).reshape(128, -1).astype(BF)
def act(Z):
    return [np.maximum(z, 0) * C for z in Z]
def pk(c, s, i=0):
    return (np.ascontiguousarray(c[:, 512 * i:512 * i + 512]), mx_ref.live(s[:, 128 * i:128 * i + 128]))
def inputs(rng, e, E):
    def f(*shape):
        v = (rng.standard_normal(shape, dtype=np.float32) * np.exp2(rng.integers(-2, 3, shape[:-1] + (1,)))).astype(BF)
        return mx_ref.spread((v.astype(np.float32) * np.exp2(rng.integers(-E, E + 1, shape[:-2] + (1, 1))).astype(np.float32)).astype(BF), rng, e)
    def packed(k):
        c = np.zeros((N, 128, k * 512), np.uint8); s = np.zeros((N, 128, k * 128), np.uint8)
        for r in range(N):
            for i in range(k):
                a, b = mx_ref.quantize(f(128, 512)); c[r][:, 512 * i:512 * i + 512] = a; s[r][:, 128 * i:128 * i + 128] = mx_ref.plane(b, rng)
        return c, s
    d = {}
    d["ac"], d["az"] = packed(1)
    d["bc"], d["bs"] = packed(1)
    d["cc"], d["cs"] = packed(1)
    d["x"] = f(N, 128, 4 * NC)
    return d
def setup_inputs(rng):
    return inputs(rng, 0, 0)
def setup_inputs_blocks(rng):
    return inputs(rng, 2, 0)
def setup_inputs_wide(rng):
    return inputs(rng, 0, 4)
def reference(ac, az, bc, bs, cc, cs, x):
    y = np.zeros((N, 128, N * NC), np.float32)
    for r in range(N):
        h = mx_ref.quantize(tile(act([mx_ref.matmul(pk(ac[i], az[i]), mx_ref.quantize(x[r])) for i in range(G)])))
        h = mx_ref.quantize(tile(act([mx_ref.matmul(pk(bc[i], bs[i]), h) for i in range(G)])))
        for j in range(N):
            y[r][:, NC * j:NC * j + NC] = mx_ref.matmul(pk(cc[j], cs[j]), h)
    return {"y": y}

@@ -1,0 +1,292 @@
+from concourse.bass import DstId, RemoteDMATransfer
+from concourse.mybir import dt, AluOpType
+
+N = 9
+G = 4
+W = 128
+NSLOT = {"A": 1, "B": 1, "C": 2}
+NPLANE = {"A": 2, "B": 2, "C": 2}
+NY = 2
+COEF = 0.041
+CORES_ALL = 512
+EA, EH = 8, 4
+FIRST = {0: [4, 1], 1: [5, 2], 2: [3, 0]}
+
+PIECES = ["A%d" % i for i in range(G)] + ["B%d" % i for i in range(G)] + ["C%d" % i for i in range(N)]
+INPUTS = {"A": ("ac", "az"), "B": ("bc", "bs"), "C": ("cc", "cs")}
+MOVING = {"A": "x", "B": "g", "C": "h"}
+
+SCRATCH = {
+    "yb": ("sbuf", [128, NY * W], "float32"),
+    "ps": ("psum", [128, 4096], "float32"),
+}
+for _l in "xgh":
+    SCRATCH["t" + _l] = ("sbuf", [128, 4 * W], "bfloat16")
+    SCRATCH["q" + _l] = ("sbuf", [128, W], "float8_e4m3fn_x4")
+    SCRATCH["p" + _l] = ("sbuf", [128, W], "uint8")
+for _l in "ABC":
+    SCRATCH["w" + _l] = ("sbuf", [128, NSLOT[_l] * W], "float8_e4m3fn_x4")
+    SCRATCH["s" + _l] = ("sbuf", [128, NPLANE[_l] * W], "uint8")
+for _p in PIECES:
+    SCRATCH["c" + _p] = ("dram", [128, W], "float8_e4m3fn_x4")
+    SCRATCH["z" + _p] = ("dram", [128, W], "uint8")
+
+SEMAPHORES = ([k + p for k in ("r", "rz", "l", "lz", "m") for p in PIECES]
+              + [k + l for k in ("o", "oz") for l in "ABC"] + ["a%s%d" % (l, i) for l in "AB" for i in range(G)]
+              + ["xl", "xq", "gq", "hq", "sent"] + [k + str(i) for k in ("cp", "st") for i in range(N)])
+
+CACHE = {}
+
+
+def engines(mask):
+    return [e for e in range(16) if mask >> e & 1]
+
+
+def submask(es):
+    m = 0
+    for e in es:
+        m |= 1 << e
+    return m
+
+
+def rot(l, k):
+    return l[k % len(l):] + l[:k % len(l)]
+
+
+def plan(T, topo):
+    if "sends" in CACHE:
+        return CACHE
+    cores = list(T.cores)
+    place = {}
+    for c in range(CORES_ALL):
+        place.setdefault((topo.host(c), topo.chip(c)), []).append(c)
+
+    def chipcores(c):
+        return place[(topo.host(c), topo.chip(c))]
+
+    def helpers(c):
+        other = [d for d in chipcores(c) if topo.die(d) != topo.die(c)]
+        return other[0], other[2], other[3]
+
+    def across(c):
+        for (h, k), l in place.items():
+            d = l[chipcores(c).index(c)]
+            if k == topo.chip(c) and topo.rack(h) != topo.rack(topo.host(c)) and topo.may_write(c, d):
+                return d
+
+    def rackof(c):
+        return topo.rack(topo.host(c))
+
+    near = [c for c in cores if rackof(c) == rackof(cores[0])]
+    far = [c for c in cores if c not in near]
+    border = [c for c in near if topo.may_write(c, far[0])]
+    inner = [c for c in near if c not in border]
+    sends = {}
+    peersof = {}
+
+    def send(c, p, dsts, part=None):
+        es = 0xFFFF
+        for d in dsts:
+            es &= topo.mask(c, d)
+        es = engines(es)
+        if part is None:
+            es = es[:EA]
+        else:
+            es = es[8 + part * EH:8 + (part + 1) * EH]
+        if part:
+            sends[c][-1].append((p, dsts, es))
+        else:
+            sends.setdefault(c, []).append([(p, dsts, es)])
+
+    for s, c in enumerate(cores):
+        peers = rot([d for d in cores if d != c and rackof(d) == rackof(c)], s)
+        if s in FIRST:
+            head = [cores[k] for k in FIRST[s]]
+            peers = head + [d for d in peers if d not in head]
+        peersof[c] = peers
+        h1, h2, h3 = helpers(c)
+        if s < G:
+            a = "A%d" % s
+            if c in inner:
+                rel = across(c)
+                send(c, a, [rel] + peers)
+                send(rel, a, rot(far, s))
+            else:
+                send(c, a, rot(far, s) + peers)
+        for n, l in enumerate("BC" if s < G else "C"):
+            p = l + str(s)
+            send(c, p, [h1, h2], part=n)
+            if c in inner:
+                rel = across(h1)
+                send(h1, p, [rel] + peers[:2])
+                send(h2, p, peers[2:])
+                send(rel, p, rot(far, s))
+            elif c in border:
+                send(h1, p, rot(far, s) + peers[:1])
+                send(h2, p, peers[1:])
+            else:
+                j = far.index(c)
+                hop = helpers(border[j])[2]
+                send(h1, p, [hop] + rot(border, j))
+                send(h2, p, peers)
+                send(hop, p, inner)
+    got = {}
+    for c, calls in sends.items():
+        for p, dsts, es in sum(calls, []):
+            for d in dsts:
+                assert (d, p) not in got, (d, p)
+                got[(d, p)] = len(es)
+    CACHE.update(sends=sends, got=got, near=near, far=far, border=border, peers=peersof)
+    return CACHE
+
+
+def order(T, topo, core):
+    P = plan(T, topo)
+    cores = list(T.cores)
+    far = core in P["far"]
+
+    def key(s):
+        c = cores[s]
+        if c == core:
+            return (0, 0)
+        if far:
+            return (1 if c in P["far"] else 2 if topo.may_write(c, core) else 3, (P["far"].index(core) - s) % 3)
+        if c in P["near"]:
+            return (1 if s >= G else 3 if c in P["border"] else 2, P["peers"][c].index(core))
+        return (2, s)
+    return {"A": sorted(range(G), key=key), "B": sorted(range(G), key=key), "C": sorted(range(N), key=key)}
+
+
+def direct(T, topo, core):
+    r = T.rank_of(core)
+    if r is None or r < G:
+        return None
+    return "A%d" % order(T, topo, core)["A"][0]
+
+
+def where(T, topo, core, p):
+    if p == direct(T, topo, core):
+        return T["wA"][:, 0:W].bitcast(dt.uint8), T["sA"][:, 0:W]
+    return T["c" + p][:].bitcast(dt.uint8), T["z" + p][:]
+
+
+def rank_program(g, core, T, topo):
+    P = plan(T, topo)
+    rank = T.rank_of(core)
+    calls = P["sends"].get(core, [])
+    if rank is None and not calls:
+        return
+    own = []
+    if rank is not None:
+        own = ["%s%d" % (l, rank) for l in ("ABC" if rank < G else "C")]
+
+    seen = set()
+    sent = 0
+    for call in calls:
+        for k, z in ((1, "z"), (0, "")):
+            trs = []
+            for p, dsts, es in call:
+                if (p, k) not in seen:
+                    seen.add((p, k))
+                    if p in own:
+                        g.wait_ge(T.sem["o" + z + p[0]], 16)
+                    else:
+                        g.wait_ge(T.sem["r" + z + p], P["got"][(core, p)])
+                ids = []
+                for d in dsts:
+                    rid, pid = topo.addr(d, core)
+                    ids.append(DstId(rid=rid, pnc=pid))
+                trs.append(RemoteDMATransfer(dst_ids=ids, dma_engine_mask=submask(es), remote_sem=T.sem["r" + z + p], alu_op=0,
+                                             srcs=[where(T, topo, core, p)[k]], dsts=[where(T, topo, d, p)[k] for d in dsts]))
+                sent += len(es)
+            g.remote_dma_fused(trs, local_sem=T.sem.sent)
+    if rank is None:
+        g.wait_ge(T.sem.sent, sent)
+        return
+
+    O = order(T, topo, core)
+    D = direct(T, topo, core)
+
+    def inp(p):
+        return T[INPUTS[p[0]][0]][:], T[INPUTS[p[0]][1]][:]
+
+    for k, z in ((1, "z"), (0, "")):
+        for p in own:
+            g.sync.dma_start(where(T, topo, core, p)[k], inp(p)[k]).then_inc(T.sem["o" + z + p[0]], 16)
+    g.scalar.dma_start(T.tx[:], T.x[:]).then_inc(T.sem.xl, 16)
+    g.vector.wait_ge(T.sem.xl, 16)
+    g.vector.quantize_mx(T.qx[:], T.px[:], T.tx[:]).then_inc(T.sem.xq, 1)
+
+    def view(p, k):
+        l, i = p[0], O[p[0]].index(int(p[1]))
+        n = i % (NPLANE if k else NSLOT)[l]
+        return T[("s" if k else "w") + l][:, n * W:(n + 1) * W]
+
+    def load(ld, p, k):
+        l, i = p[0], O[p[0]].index(int(p[1]))
+        z = "z" if k else ""
+        if p == D:
+            return
+        m = (NPLANE if k else NSLOT)[l]
+        if i >= m:
+            ld.wait_ge(T.sem["m%s%d" % (l, O[l][i - m])], 1)
+        if p in own:
+            src = inp(p)[k]
+        else:
+            ld.wait_ge(T.sem["r" + z + p], P["got"][(core, p)])
+            src = where(T, topo, core, p)[k]
+        ld.dma_start(view(p, k) if k else view(p, k).bitcast(dt.uint8), src).then_inc(T.sem["l" + z + p], 16)
+
+    for l in "ABC":
+        ahead = NPLANE[l] - NSLOT[l]
+        ps = ["%s%d" % (l, s) for s in O[l]]
+        for i, p in enumerate(ps):
+            ld = g.scalar if l == "B" or (l == "C" and i >= NSLOT[l]) else g.sync
+            if i == 0:
+                for n in range(ahead):
+                    load(ld, ps[n], 1)
+            if i + ahead < len(ps) and not ahead:
+                load(ld, ps[i], 1)
+            load(ld, p, 0)
+            if i + ahead < len(ps) and ahead:
+                load(ld, ps[i + ahead], 1)
+
+    def mm(p, bank):
+        l = p[0]
+        for z in ("z", ""):
+            if p == D:
+                g.tensor.wait_ge(T.sem["r" + z + p], P["got"][(core, p)])
+            else:
+                g.tensor.wait_ge(T.sem["l" + z + p], 16)
+        g.tensor.matmul_mx(T.ps[:, 512 * bank:512 * bank + W], view(p, 0), view(p, 1),
+                           T["q" + MOVING[l]][:], T["p" + MOVING[l]][:], True, True).then_inc(T.sem["m" + p], 1)
+
+    for l, base, m in (("A", 0, "g"), ("B", 4, "h")):
+        g.tensor.wait_ge(T.sem[MOVING[l] + "q"], 1)
+        for s in O[l]:
+            p = "%s%d" % (l, s)
+            mm(p, base + s)
+            g.vector.wait_ge(T.sem["m" + p], 1)
+            g.vector.tensor_scalar(T["t" + m][:, s:4 * W:4], T.ps[:, 512 * (base + s):512 * (base + s) + W],
+                                   0.0, COEF, AluOpType.max, AluOpType.mult).then_inc(T.sem["a" + p], 1)
+        for s in O[l]:
+            g.vector.wait_ge(T.sem["a%s%d" % (l, s)], 1)
+        g.vector.quantize_mx(T["q" + m][:], T["p" + m][:], T["t" + m][:]).then_inc(T.sem[m + "q"], 1)
+
+    g.tensor.wait_ge(T.sem.hq, 1)
+    for k, s in enumerate(O["C"]):
+        p = "C%d" % s
+        bank = k % 8
+        if k >= 8:
+            g.tensor.wait_ge(T.sem["cp%d" % (k - 8)], 1)
+        mm(p, bank)
+        n = k % NY
+        if k >= NY:
+            g.vector.wait_ge(T.sem["st%d" % (k - NY)], 16)
+        g.vector.wait_ge(T.sem["m" + p], 1)
+        g.vector.tensor_copy(T.yb[:, n * W:(n + 1) * W], T.ps[:, 512 * bank:512 * bank + W]).then_inc(T.sem["cp%d" % k], 1)
+        g.sync.wait_ge(T.sem["cp%d" % k], 1)
+        g.sync.dma_start(T.y[:, s * W:(s + 1) * W], T.yb[:, n * W:(n + 1) * W]).then_inc(T.sem["st%d" % k], 16)
+    for k in range(N):
+        g.sync.wait_ge(T.sem["st%d" % k], 16)
+    g.wait_ge(T.sem.sent, sent)

@@ -4,9 +4,9 @@ from concourse.mybir import dt, AluOpType
 N = 9
 G = 4
 W = 128
-NSLOT = {"A": 1, "B": 1, "C": 2}
-NPLANE = {"A": 2, "B": 2, "C": 2}
-NY = 2
+NSLOT = {"A": 1, "B": 2, "C": 3}
+NPLANE = {"A": 2, "B": 2, "C": 3}
+NY = 3
 COEF = 0.041
 CORES_ALL = 512
 EA, EH = 8, 4
@@ -15,12 +15,19 @@ FIRST = {0: [4, 1], 1: [5, 2], 2: [3, 0]}
 PIECES = ["A%d" % i for i in range(G)] + ["B%d" % i for i in range(G)] + ["C%d" % i for i in range(N)]
 INPUTS = {"A": ("ac", "az"), "B": ("bc", "bs"), "C": ("cc", "cs")}
 MOVING = {"A": "x", "B": "g", "C": "h"}
+BUF = {"x": "x", "g": "g", "h": "g"}
+
+TAKE = {
+    "A": ["0321", "1032", "2103", "3210", "3021", "3120", "0213", "1023", "2103"],
+    "B": ["0312", "1203", "2013", "3102", "2103", "1203", "0321", "1032", "2103"],
+    "C": ["054623187", "154607238", "254610873", "354261087", "450632187", "541632087", "687540321", "768451032", "876542103"],
+}
 
 SCRATCH = {
     "yb": ("sbuf", [128, NY * W], "float32"),
     "ps": ("psum", [128, 4096], "float32"),
 }
-for _l in "xgh":
+for _l in "xg":
     SCRATCH["t" + _l] = ("sbuf", [128, 4 * W], "bfloat16")
     SCRATCH["q" + _l] = ("sbuf", [128, W], "float8_e4m3fn_x4")
     SCRATCH["p" + _l] = ("sbuf", [128, W], "uint8")
@@ -64,10 +71,6 @@ def plan(T, topo):
     def chipcores(c):
         return place[(topo.host(c), topo.chip(c))]
 
-    def helpers(c):
-        other = [d for d in chipcores(c) if topo.die(d) != topo.die(c)]
-        return other[0], other[2], other[3]
-
     def across(c):
         for (h, k), l in place.items():
             d = l[chipcores(c).index(c)]
@@ -79,93 +82,70 @@ def plan(T, topo):
 
     near = [c for c in cores if rackof(c) == rackof(cores[0])]
     far = [c for c in cores if c not in near]
-    border = [c for c in near if topo.may_write(c, far[0])]
-    inner = [c for c in near if c not in border]
     sends = {}
-    peersof = {}
 
-    def send(c, p, dsts, part=None):
+    def part(c, p, dsts, lo=0, n=EA):
         es = 0xFFFF
         for d in dsts:
             es &= topo.mask(c, d)
-        es = engines(es)
-        if part is None:
-            es = es[:EA]
-        else:
-            es = es[8 + part * EH:8 + (part + 1) * EH]
-        if part:
-            sends[c][-1].append((p, dsts, es))
-        else:
-            sends.setdefault(c, []).append([(p, dsts, es)])
+        return (p, dsts, engines(es)[lo:lo + n])
+
+    def both(c, *parts):
+        for what in "zc":
+            sends.setdefault(c, []).append((what, list(parts)))
 
     for s, c in enumerate(cores):
         peers = rot([d for d in cores if d != c and rackof(d) == rackof(c)], s)
         if s in FIRST:
             head = [cores[k] for k in FIRST[s]]
             peers = head + [d for d in peers if d not in head]
-        peersof[c] = peers
-        h1, h2, h3 = helpers(c)
-        if s < G:
-            a = "A%d" % s
-            if c in inner:
-                rel = across(c)
-                send(c, a, [rel] + peers)
-                send(rel, a, rot(far, s))
-            else:
-                send(c, a, rot(far, s) + peers)
-        for n, l in enumerate("BC" if s < G else "C"):
-            p = l + str(s)
-            send(c, p, [h1, h2], part=n)
-            if c in inner:
-                rel = across(h1)
-                send(h1, p, [rel] + peers[:2])
-                send(h2, p, peers[2:])
-                send(rel, p, rot(far, s))
-            elif c in border:
-                send(h1, p, rot(far, s) + peers[:1])
-                send(h2, p, peers[1:])
-            else:
-                j = far.index(c)
-                hop = helpers(border[j])[2]
-                send(h1, p, [hop] + rot(border, j))
-                send(h2, p, peers)
-                send(hop, p, inner)
+        beyond = rot(far if c in near else near, s)
+        mine = [d for d in chipcores(c) if d != c and topo.die(d) == topo.die(c)]
+        other = [d for d in chipcores(c) if topo.die(d) != topo.die(c)]
+        a, b, k = "A%d" % s, "B%d" % s, "C%d" % s
+        if s >= G:
+            h1, h2 = mine[1], mine[2]
+            rel = across(h1)
+            both(c, part(c, k, [h1, h2], 8, EH))
+            both(h1, part(h1, k, [rel]))
+            both(h2, part(h2, k, peers))
+            both(rel, part(rel, k, beyond))
+            continue
+        h1, h2 = other[0], other[2]
+        if topo.may_write(c, beyond[0]):
+            h3 = mine[0]
+            rel = across(h3)
+            both(c, part(c, a, peers))
+            both(c, part(c, a, [h3], 8, EH), part(c, b, [h1, h2], 12, 2), part(c, k, [h1, h2], 14, 2))
+            both(h3, part(h3, a, [rel]))
+        else:
+            rel = across(c)
+            both(c, part(c, a, [rel] + peers))
+            both(c, part(c, b, [h1, h2], 8, EH), part(c, k, [h1, h2], 8 + EH, EH))
+        both(rel, part(rel, a, beyond))
+        both(h1, part(h1, b, [across(h1)] + peers[:2]))
+        both(h2, part(h2, b, peers[2:]))
+        both(across(h1), part(across(h1), b, beyond))
+        both(h1, part(h1, k, peers[:2]))
+        both(h2, part(h2, k, [across(h2)] + peers[2:]))
+        both(across(h2), part(across(h2), k, beyond))
     got = {}
     for c, calls in sends.items():
-        for p, dsts, es in sum(calls, []):
-            for d in dsts:
-                assert (d, p) not in got, (d, p)
-                got[(d, p)] = len(es)
-    CACHE.update(sends=sends, got=got, near=near, far=far, border=border, peers=peersof)
+        for what, parts in calls:
+            for p, dsts, es in parts:
+                for d in dsts:
+                    got[(d, p)] = len(es)
+    CACHE.update(sends=sends, got=got)
     return CACHE
 
 
-def order(T, topo, core):
-    P = plan(T, topo)
-    cores = list(T.cores)
-    far = core in P["far"]
-
-    def key(s):
-        c = cores[s]
-        if c == core:
-            return (0, 0)
-        if far:
-            return (1 if c in P["far"] else 2 if topo.may_write(c, core) else 3, (P["far"].index(core) - s) % 3)
-        if c in P["near"]:
-            return (1 if s >= G else 3 if c in P["border"] else 2, P["peers"][c].index(core))
-        return (2, s)
-    return {"A": sorted(range(G), key=key), "B": sorted(range(G), key=key), "C": sorted(range(N), key=key)}
-
-
-def direct(T, topo, core):
+def direct(T, core):
     r = T.rank_of(core)
-    if r is None or r < G:
-        return None
-    return "A%d" % order(T, topo, core)["A"][0]
+    return None if r is None or r < G else "A" + TAKE["A"][r][0]
 
 
-def where(T, topo, core, p):
-    if p == direct(T, topo, core):
+def where(T, core, p):
+    if p == direct(T, core):
         return T["wA"][:, 0:W].bitcast(dt.uint8), T["sA"][:, 0:W]
     return T["c" + p][:].bitcast(dt.uint8), T["z" + p][:]
 
@@ -179,103 +159,102 @@ def rank_program(g, core, T, topo):
     own = []
     if rank is not None:
         own = ["%s%d" % (l, rank) for l in ("ABC" if rank < G else "C")]
+    D = direct(T, core)
 
     seen = set()
     sent = 0
-    for call in calls:
-        for k, z in ((1, "z"), (0, "")):
-            trs = []
-            for p, dsts, es in call:
-                if (p, k) not in seen:
-                    seen.add((p, k))
-                    if p in own:
-                        g.wait_ge(T.sem["o" + z + p[0]], 16)
-                    else:
-                        g.wait_ge(T.sem["r" + z + p], P["got"][(core, p)])
-                ids = []
-                for d in dsts:
-                    rid, pid = topo.addr(d, core)
-                    ids.append(DstId(rid=rid, pnc=pid))
-                trs.append(RemoteDMATransfer(dst_ids=ids, dma_engine_mask=submask(es), remote_sem=T.sem["r" + z + p], alu_op=0,
-                                             srcs=[where(T, topo, core, p)[k]], dsts=[where(T, topo, d, p)[k] for d in dsts]))
-                sent += len(es)
-            g.remote_dma_fused(trs, local_sem=T.sem.sent)
+    for what, parts in calls:
+        k, z = (1, "z") if what == "z" else (0, "")
+        trs = []
+        for p, dsts, es in parts:
+            if (p, k) not in seen:
+                seen.add((p, k))
+                if p in own:
+                    g.wait_ge(T.sem["o" + z + p[0]], 16)
+                else:
+                    g.wait_ge(T.sem["r" + z + p], P["got"][(core, p)])
+            ids = []
+            for d in dsts:
+                rid, pid = topo.addr(d, core)
+                ids.append(DstId(rid=rid, pnc=pid))
+            trs.append(RemoteDMATransfer(dst_ids=ids, dma_engine_mask=submask(es), remote_sem=T.sem["r" + z + p], alu_op=0,
+                                         srcs=[where(T, core, p)[k]], dsts=[where(T, d, p)[k] for d in dsts]))
+            sent += len(es)
+        g.remote_dma_fused(trs, local_sem=T.sem.sent)
     if rank is None:
         g.wait_ge(T.sem.sent, sent)
         return
 
-    O = order(T, topo, core)
-    D = direct(T, topo, core)
+    take = {l: [l + s for s in TAKE[l][rank]] for l in "ABC"}
 
     def inp(p):
         return T[INPUTS[p[0]][0]][:], T[INPUTS[p[0]][1]][:]
 
     for k, z in ((1, "z"), (0, "")):
         for p in own:
-            g.sync.dma_start(where(T, topo, core, p)[k], inp(p)[k]).then_inc(T.sem["o" + z + p[0]], 16)
+            g.sync.dma_start(where(T, core, p)[k], inp(p)[k]).then_inc(T.sem["o" + z + p[0]], 16)
     g.scalar.dma_start(T.tx[:], T.x[:]).then_inc(T.sem.xl, 16)
     g.vector.wait_ge(T.sem.xl, 16)
     g.vector.quantize_mx(T.qx[:], T.px[:], T.tx[:]).then_inc(T.sem.xq, 1)
 
     def view(p, k):
-        l, i = p[0], O[p[0]].index(int(p[1]))
-        n = i % (NPLANE if k else NSLOT)[l]
+        l = p[0]
+        n = take[l].index(p) % (NPLANE if k else NSLOT)[l]
         return T[("s" if k else "w") + l][:, n * W:(n + 1) * W]
 
     def load(ld, p, k):
-        l, i = p[0], O[p[0]].index(int(p[1]))
+        l, i = p[0], take[p[0]].index(p)
         z = "z" if k else ""
         if p == D:
             return
         m = (NPLANE if k else NSLOT)[l]
         if i >= m:
-            ld.wait_ge(T.sem["m%s%d" % (l, O[l][i - m])], 1)
+            ld.wait_ge(T.sem["m" + take[l][i - m]], 1)
         if p in own:
             src = inp(p)[k]
         else:
             ld.wait_ge(T.sem["r" + z + p], P["got"][(core, p)])
-            src = where(T, topo, core, p)[k]
+            src = where(T, core, p)[k]
         ld.dma_start(view(p, k) if k else view(p, k).bitcast(dt.uint8), src).then_inc(T.sem["l" + z + p], 16)
 
     for l in "ABC":
+        ld = g.sync if l == "A" else g.scalar
         ahead = NPLANE[l] - NSLOT[l]
-        ps = ["%s%d" % (l, s) for s in O[l]]
-        for i, p in enumerate(ps):
-            ld = g.scalar if l == "B" or (l == "C" and i >= NSLOT[l]) else g.sync
-            if i == 0:
-                for n in range(ahead):
-                    load(ld, ps[n], 1)
-            if i + ahead < len(ps) and not ahead:
-                load(ld, ps[i], 1)
+        for p in take[l][:ahead]:
+            load(ld, p, 1)
+        for i, p in enumerate(take[l]):
+            if not ahead:
+                load(ld, p, 1)
             load(ld, p, 0)
-            if i + ahead < len(ps) and ahead:
-                load(ld, ps[i + ahead], 1)
+            if ahead and i + ahead < len(take[l]):
+                load(ld, take[l][i + ahead], 1)
 
     def mm(p, bank):
-        l = p[0]
         for z in ("z", ""):
             if p == D:
                 g.tensor.wait_ge(T.sem["r" + z + p], P["got"][(core, p)])
             else:
                 g.tensor.wait_ge(T.sem["l" + z + p], 16)
+        m = BUF[MOVING[p[0]]]
         g.tensor.matmul_mx(T.ps[:, 512 * bank:512 * bank + W], view(p, 0), view(p, 1),
-                           T["q" + MOVING[l]][:], T["p" + MOVING[l]][:], True, True).then_inc(T.sem["m" + p], 1)
+                           T["q" + m][:], T["p" + m][:], True, True).then_inc(T.sem["m" + p], 1)
 
     for l, base, m in (("A", 0, "g"), ("B", 4, "h")):
         g.tensor.wait_ge(T.sem[MOVING[l] + "q"], 1)
-        for s in O[l]:
-            p = "%s%d" % (l, s)
+        u = BUF[m]
+        for p in take[l]:
+            s = int(p[1])
             mm(p, base + s)
             g.vector.wait_ge(T.sem["m" + p], 1)
-            g.vector.tensor_scalar(T["t" + m][:, s:4 * W:4], T.ps[:, 512 * (base + s):512 * (base + s) + W],
+            g.vector.tensor_scalar(T["t" + u][:, s:4 * W:4], T.ps[:, 512 * (base + s):512 * (base + s) + W],
                                    0.0, COEF, AluOpType.max, AluOpType.mult).then_inc(T.sem["a" + p], 1)
-        for s in O[l]:
-            g.vector.wait_ge(T.sem["a%s%d" % (l, s)], 1)
-        g.vector.quantize_mx(T["q" + m][:], T["p" + m][:], T["t" + m][:]).then_inc(T.sem[m + "q"], 1)
+        for p in take[l]:
+            g.vector.wait_ge(T.sem["a" + p], 1)
+        g.vector.quantize_mx(T["q" + u][:], T["p" + u][:], T["t" + u][:]).then_inc(T.sem[m + "q"], 1)
 
     g.tensor.wait_ge(T.sem.hq, 1)
-    for k, s in enumerate(O["C"]):
-        p = "C%d" % s
+    for k, p in enumerate(take["C"]):
+        s = int(p[1])
         bank = k % 8
         if k >= 8:
             g.tensor.wait_ge(T.sem["cp%d" % (k - 8)], 1)

from concourse.bass import DstId, RemoteDMATransfer
from concourse.mybir import dt, AluOpType

N = 9
G = 4
W = 128
NSLOT = {"A": 1, "B": 2, "C": 3}
NPLANE = {"A": 2, "B": 2, "C": 3}
NY = 3
COEF = 0.041
CORES_ALL = 512
EA, EH = 8, 4
FIRST = {0: [4, 1], 1: [5, 2], 2: [3, 0]}

PIECES = ["A%d" % i for i in range(G)] + ["B%d" % i for i in range(G)] + ["C%d" % i for i in range(N)]
INPUTS = {"A": ("ac", "az"), "B": ("bc", "bs"), "C": ("cc", "cs")}
MOVING = {"A": "x", "B": "g", "C": "h"}
BUF = {"x": "x", "g": "g", "h": "g"}

TAKE = {
    "A": ["0321", "1032", "2103", "3210", "3021", "3120", "0213", "1023", "2103"],
    "B": ["0312", "1203", "2013", "3102", "2103", "1203", "0321", "1032", "2103"],
    "C": ["054623187", "154607238", "254610873", "354261087", "450632187", "541632087", "687540321", "768451032", "876542103"],
}

SCRATCH = {
    "yb": ("sbuf", [128, NY * W], "float32"),
    "ps": ("psum", [128, 4096], "float32"),
}
for _l in "xg":
    SCRATCH["t" + _l] = ("sbuf", [128, 4 * W], "bfloat16")
    SCRATCH["q" + _l] = ("sbuf", [128, W], "float8_e4m3fn_x4")
    SCRATCH["p" + _l] = ("sbuf", [128, W], "uint8")
for _l in "ABC":
    SCRATCH["w" + _l] = ("sbuf", [128, NSLOT[_l] * W], "float8_e4m3fn_x4")
    SCRATCH["s" + _l] = ("sbuf", [128, NPLANE[_l] * W], "uint8")
for _p in PIECES:
    SCRATCH["c" + _p] = ("dram", [128, W], "float8_e4m3fn_x4")
    SCRATCH["z" + _p] = ("dram", [128, W], "uint8")

SEMAPHORES = ([k + p for k in ("r", "rz", "l", "lz", "m") for p in PIECES]
              + [k + l for k in ("o", "oz") for l in "ABC"] + ["a%s%d" % (l, i) for l in "AB" for i in range(G)]
              + ["xl", "xq", "gq", "hq", "sent"] + [k + str(i) for k in ("cp", "st") for i in range(N)])

CACHE = {}


def engines(mask):
    return [e for e in range(16) if mask >> e & 1]


def submask(es):
    m = 0
    for e in es:
        m |= 1 << e
    return m


def rot(l, k):
    return l[k % len(l):] + l[:k % len(l)]


def plan(T, topo):
    if "sends" in CACHE:
        return CACHE
    cores = list(T.cores)
    place = {}
    for c in range(CORES_ALL):
        place.setdefault((topo.host(c), topo.chip(c)), []).append(c)

    def chipcores(c):
        return place[(topo.host(c), topo.chip(c))]

    def across(c):
        for (h, k), l in place.items():
            d = l[chipcores(c).index(c)]
            if k == topo.chip(c) and topo.rack(h) != topo.rack(topo.host(c)) and topo.may_write(c, d):
                return d

    def rackof(c):
        return topo.rack(topo.host(c))

    near = [c for c in cores if rackof(c) == rackof(cores[0])]
    far = [c for c in cores if c not in near]
    sends = {}

    def part(c, p, dsts, lo=0, n=EA):
        es = 0xFFFF
        for d in dsts:
            es &= topo.mask(c, d)
        return (p, dsts, engines(es)[lo:lo + n])

    def both(c, *parts):
        for what in "zc":
            sends.setdefault(c, []).append((what, list(parts)))

    for s, c in enumerate(cores):
        peers = rot([d for d in cores if d != c and rackof(d) == rackof(c)], s)
        if s in FIRST:
            head = [cores[k] for k in FIRST[s]]
            peers = head + [d for d in peers if d not in head]
        beyond = rot(far if c in near else near, s)
        mine = [d for d in chipcores(c) if d != c and topo.die(d) == topo.die(c)]
        other = [d for d in chipcores(c) if topo.die(d) != topo.die(c)]
        a, b, k = "A%d" % s, "B%d" % s, "C%d" % s
        if s >= G:
            h1, h2 = mine[1], mine[2]
            rel = across(h1)
            both(c, part(c, k, [h1, h2], 8, EH))
            both(h1, part(h1, k, [rel]))
            both(h2, part(h2, k, peers))
            both(rel, part(rel, k, beyond))
            continue
        h1, h2 = other[0], other[2]
        if topo.may_write(c, beyond[0]):
            h3 = mine[0]
            rel = across(h3)
            both(c, part(c, a, peers))
            both(c, part(c, a, [h3], 8, EH), part(c, b, [h1, h2], 12, 2), part(c, k, [h1, h2], 14, 2))
            both(h3, part(h3, a, [rel]))
        else:
            rel = across(c)
            both(c, part(c, a, [rel] + peers))
            both(c, part(c, b, [h1, h2], 8, EH), part(c, k, [h1, h2], 8 + EH, EH))
        both(rel, part(rel, a, beyond))
        both(h1, part(h1, b, [across(h1)] + peers[:2]))
        both(h2, part(h2, b, peers[2:]))
        both(across(h1), part(across(h1), b, beyond))
        both(h1, part(h1, k, peers[:2]))
        both(h2, part(h2, k, [across(h2)] + peers[2:]))
        both(across(h2), part(across(h2), k, beyond))
    got = {}
    for c, calls in sends.items():
        for what, parts in calls:
            for p, dsts, es in parts:
                for d in dsts:
                    got[(d, p)] = len(es)
    CACHE.update(sends=sends, got=got)
    return CACHE


def direct(T, core):
    r = T.rank_of(core)
    return None if r is None or r < G else "A" + TAKE["A"][r][0]


def where(T, core, p):
    if p == direct(T, core):
        return T["wA"][:, 0:W].bitcast(dt.uint8), T["sA"][:, 0:W]
    return T["c" + p][:].bitcast(dt.uint8), T["z" + p][:]


def rank_program(g, core, T, topo):
    P = plan(T, topo)
    rank = T.rank_of(core)
    calls = P["sends"].get(core, [])
    if rank is None and not calls:
        return
    own = []
    if rank is not None:
        own = ["%s%d" % (l, rank) for l in ("ABC" if rank < G else "C")]
    D = direct(T, core)

    seen = set()
    sent = 0
    for what, parts in calls:
        k, z = (1, "z") if what == "z" else (0, "")
        trs = []
        for p, dsts, es in parts:
            if (p, k) not in seen:
                seen.add((p, k))
                if p in own:
                    g.wait_ge(T.sem["o" + z + p[0]], 16)
                else:
                    g.wait_ge(T.sem["r" + z + p], P["got"][(core, p)])
            ids = []
            for d in dsts:
                rid, pid = topo.addr(d, core)
                ids.append(DstId(rid=rid, pnc=pid))
            trs.append(RemoteDMATransfer(dst_ids=ids, dma_engine_mask=submask(es), remote_sem=T.sem["r" + z + p], alu_op=0,
                                         srcs=[where(T, core, p)[k]], dsts=[where(T, d, p)[k] for d in dsts]))
            sent += len(es)
        g.remote_dma_fused(trs, local_sem=T.sem.sent)
    if rank is None:
        g.wait_ge(T.sem.sent, sent)
        return

    take = {l: [l + s for s in TAKE[l][rank]] for l in "ABC"}

    def inp(p):
        return T[INPUTS[p[0]][0]][:], T[INPUTS[p[0]][1]][:]

    for k, z in ((1, "z"), (0, "")):
        for p in own:
            g.sync.dma_start(where(T, core, p)[k], inp(p)[k]).then_inc(T.sem["o" + z + p[0]], 16)
    g.scalar.dma_start(T.tx[:], T.x[:]).then_inc(T.sem.xl, 16)
    g.vector.wait_ge(T.sem.xl, 16)
    g.vector.quantize_mx(T.qx[:], T.px[:], T.tx[:]).then_inc(T.sem.xq, 1)

    def view(p, k):
        l = p[0]
        n = take[l].index(p) % (NPLANE if k else NSLOT)[l]
        return T[("s" if k else "w") + l][:, n * W:(n + 1) * W]

    def load(ld, p, k):
        l, i = p[0], take[p[0]].index(p)
        z = "z" if k else ""
        if p == D:
            return
        m = (NPLANE if k else NSLOT)[l]
        if i >= m:
            ld.wait_ge(T.sem["m" + take[l][i - m]], 1)
        if p in own:
            src = inp(p)[k]
        else:
            ld.wait_ge(T.sem["r" + z + p], P["got"][(core, p)])
            src = where(T, core, p)[k]
        ld.dma_start(view(p, k) if k else view(p, k).bitcast(dt.uint8), src).then_inc(T.sem["l" + z + p], 16)

    for l in "ABC":
        ld = g.sync if l == "A" else g.scalar
        ahead = NPLANE[l] - NSLOT[l]
        for p in take[l][:ahead]:
            load(ld, p, 1)
        for i, p in enumerate(take[l]):
            if not ahead:
                load(ld, p, 1)
            load(ld, p, 0)
            if ahead and i + ahead < len(take[l]):
                load(ld, take[l][i + ahead], 1)

    def mm(p, bank):
        for z in ("z", ""):
            if p == D:
                g.tensor.wait_ge(T.sem["r" + z + p], P["got"][(core, p)])
            else:
                g.tensor.wait_ge(T.sem["l" + z + p], 16)
        m = BUF[MOVING[p[0]]]
        g.tensor.matmul_mx(T.ps[:, 512 * bank:512 * bank + W], view(p, 0), view(p, 1),
                           T["q" + m][:], T["p" + m][:], True, True).then_inc(T.sem["m" + p], 1)

    for l, base, m in (("A", 0, "g"), ("B", 4, "h")):
        g.tensor.wait_ge(T.sem[MOVING[l] + "q"], 1)
        u = BUF[m]
        for p in take[l]:
            s = int(p[1])
            mm(p, base + s)
            g.vector.wait_ge(T.sem["m" + p], 1)
            g.vector.tensor_scalar(T["t" + u][:, s:4 * W:4], T.ps[:, 512 * (base + s):512 * (base + s) + W],
                                   0.0, COEF, AluOpType.max, AluOpType.mult).then_inc(T.sem["a" + p], 1)
        for p in take[l]:
            g.vector.wait_ge(T.sem["a" + p], 1)
        g.vector.quantize_mx(T["q" + u][:], T["p" + u][:], T["t" + u][:]).then_inc(T.sem[m + "q"], 1)

    g.tensor.wait_ge(T.sem.hq, 1)
    for k, p in enumerate(take["C"]):
        s = int(p[1])
        bank = k % 8
        if k >= 8:
            g.tensor.wait_ge(T.sem["cp%d" % (k - 8)], 1)
        mm(p, bank)
        n = k % NY
        if k >= NY:
            g.vector.wait_ge(T.sem["st%d" % (k - NY)], 16)
        g.vector.wait_ge(T.sem["m" + p], 1)
        g.vector.tensor_copy(T.yb[:, n * W:(n + 1) * W], T.ps[:, 512 * bank:512 * bank + W]).then_inc(T.sem["cp%d" % k], 1)
        g.sync.wait_ge(T.sem["cp%d" % k], 1)
        g.sync.dma_start(T.y[:, s * W:(s + 1) * W], T.yb[:, n * W:(n + 1) * W]).then_inc(T.sem["st%d" % k], 16)
    for k in range(N):
        g.sync.wait_ge(T.sem["st%d" % k], 16)
    g.wait_ge(T.sem.sent, sent)
